import numpy as np
import ml_dtypes


def mxq(x, axis, fmt="e4m3"):
    dtype, down = {"e4m3": (ml_dtypes.float8_e4m3fn, 7), "e5m2": (ml_dtypes.float8_e5m2, 14)}[fmt]
    v = np.moveaxis(np.asarray(x, np.float32).astype(ml_dtypes.bfloat16).astype(np.float64), axis, -1)
    blocks = v.reshape(v.shape[:-1] + (-1, 32))
    amax = np.abs(blocks).max(-1, keepdims=True)
    byte = np.maximum(np.where(amax > 0, np.frexp(amax)[1] - 1 + 127, 0) - down, 1)
    scale = np.exp2(byte - 127.0)
    codes = (blocks / scale).astype(np.float32).astype(dtype).astype(np.float64)
    return np.moveaxis((codes * scale).reshape(v.shape), -1, axis)


WIDE = False


def mx_kscale(k):
    if not WIDE:
        return np.ones(k)
    levels = np.array([10, -10, 5, -5, 0])
    if k % 512:
        return np.exp2(np.random.permutation(np.resize(levels, k // 32))).repeat(32)
    a = np.empty((k // 512, 16))
    for p in range(k // 512):
        a[p, :8] = np.random.permutation(np.resize(levels, 8))
        for g in range(8):
            far = levels[np.abs(levels - a[p, g]) >= 10]
            a[p, g + 8] = far[np.random.randint(len(far))]
    return np.exp2(a.ravel()).repeat(32)


def f64(x):
    return np.asarray(x).astype(np.float64)


def striped(idx):
    return np.tile(idx.reshape(-1, 16).T, (8, 1)).astype(np.uint16)


def unstriped(offs):
    return offs[:16].T.reshape(-1).astype(np.int64)


E2M1 = np.array([0.0, 0.5, 1.0, 1.5, 2.0, 3.0, 4.0, 6.0, -0.0, -0.5, -1.0, -1.5, -2.0, -3.0, -4.0, -6.0])


def pack_weight(w, fmt):
    k, n = w.shape
    w = f64(np.asarray(w, np.float32).astype(ml_dtypes.bfloat16)).reshape(k // 32, 32, n)
    amax = np.abs(w).max(1)
    if fmt == "e4m3":
        byte = np.frexp(amax)[1] - 1 + 127 - 7
    else:
        mant, ex = np.frexp(amax / 6.0)
        byte = np.where(mant > 0.5, ex, ex - 1) + 127
    byte = np.clip(np.where(amax > 0, byte, 1), 1, 254)
    scaled = (w * np.exp2(127.0 - byte)[:, None, :]).reshape(k, n).astype(np.float32)
    by_word = np.ascontiguousarray(scaled.reshape(k // 512, 128, 4, n).transpose(0, 1, 3, 2))
    if fmt == "e4m3":
        words = by_word.astype(ml_dtypes.float8_e4m3fn).view(np.uint8)
    else:
        c = by_word.astype(ml_dtypes.float4_e2m1fn).view(np.uint8) & 0xF
        words = (c[..., 0::2] | (c[..., 1::2] << 4)).reshape(k // 512, 128, 2 * n)
    return np.ascontiguousarray(words), np.ascontiguousarray(byte.astype(np.uint8).reshape(k // 512, 16, n))


def unpack_weight(words, scales, fmt):
    g, _, n = scales.shape
    words = np.ascontiguousarray(words).reshape(g, 128, n, -1)
    if fmt == "e4m3":
        vals = words.view(ml_dtypes.float8_e4m3fn).astype(np.float64)
    else:
        nib = np.empty((g, 128, n, 4), np.uint8)
        nib[..., 0::2] = words & 0xF
        nib[..., 1::2] = words >> 4
        vals = E2M1[nib]
    vals = vals * np.repeat(np.exp2(scales.astype(np.float64) - 127.0), 8, axis=1)[..., None]
    return vals.transpose(0, 1, 3, 2).reshape(g * 512, n)


def gelu(v):
    return 0.5 * v * (1.0 + np.tanh(np.sqrt(2.0 / np.pi) * (v + 0.044715 * v**3)))


def bf(x):
    return np.asarray(x, np.float32).astype(ml_dtypes.bfloat16)


def planes(Y):
    n, m = Y.shape
    b = f64(bf(Y)).reshape(n // 32, 32, m)
    amax = np.abs(b).max(1)
    byte = np.clip(np.where(amax > 0, np.frexp(amax)[1] - 1 + 127 - 7, 1), 1, 254)
    codes = (b * np.exp2(127.0 - byte)[:, None, :]).reshape(n, m).astype(np.float32).astype(ml_dtypes.float8_e4m3fn).view(np.uint8)
    words = codes.reshape(n // 512, 128, 4, m).transpose(0, 1, 3, 2)
    return np.ascontiguousarray(words), np.ascontiguousarray(byte.astype(np.uint8).reshape(n // 512, 16, m))


K, H, N, T, T3, S, T2 = 1024, 512, 1024, 2048, 1024, 512, 1024

def setup_inputs():
    n = np.random.standard_normal
    s, u = mx_kscale(K)[:, None], mx_kscale(H)[:, None]
    size = np.exp(0.8 * n(N))
    tab_words, tab_scales = pack_weight(n((K, T)) * s, "e4m3")
    tab2_words, tab2_scales = pack_weight(n((K, T3)) * s, "e4m3")
    w2_words, w2_scales = pack_weight(n((K, H)) * 2.6 / np.sqrt(K) / s * u.T, "e2m1")
    w4_words, w4_scales = pack_weight(n((H, N)) * 0.7 / np.sqrt(H) / u * size[None, :], "e4m3")
    return {
        "tab_words": tab_words, "tab_scales": tab_scales,
        "tab2_words": tab2_words, "tab2_scales": tab2_scales,
        "offs": striped(np.random.permutation(T)[:S]),
        "offs2": striped(np.random.permutation(T3)[:S]),
        "offs3": striped(np.random.permutation(T2)[:S]),
        "offs4": striped(np.random.permutation(T2)[:S]),
        "w1": (n((K, H)) * 0.58 / np.sqrt(K) / s).astype(np.float32),
        "w2_words": w2_words, "w2_scales": w2_scales,
        "w3": (n((K, H)) * 1.6 / np.sqrt(K) / s).astype(np.float32),
        "gain": (np.random.uniform(1.0, 2.0, H) * u[:, 0]).astype(np.float32),
        "wg1": np.exp(0.3 * n((128, S))).astype(np.float32),
        "wg2": np.exp(0.3 * n((128, S))).astype(np.float32),
        "ground": (0.5 * n((H, T2)) * u).astype(np.float32),
        "w4_words": w4_words, "w4_scales": w4_scales,
        "b4": (0.5 * n(N) * size).astype(np.float32)}

def reference(tab_words, tab_scales, tab2_words, tab2_scales, offs, offs2, offs3, offs4, w1, w2_words, w2_scales, w3, gain, wg1, wg2, ground, w4_words, w4_scales, b4):
    v = unpack_weight(tab_words, tab_scales, "e4m3")[:, unstriped(offs)]
    v2 = unpack_weight(tab2_words, tab2_scales, "e4m3")[:, unstriped(offs2)]
    phase = mxq(f64(w1), 0, "e4m3").T @ v
    h1 = np.sin(phase) * (unpack_weight(w2_words, w2_scales, "e2m1").T @ v)
    h2 = f64(gain)[:, None] * np.tanh(mxq(f64(w3), 0, "e4m3").T @ v2)
    pa = np.zeros((H, T2))
    pa[:, unstriped(offs3)] = np.tile(f64(wg1), (H // 128, 1)) * h1
    pb = np.zeros((H, T2))
    pb[:, unstriped(offs4)] = np.tile(f64(wg2), (H // 128, 1)) * h2
    z = np.maximum(pa, pb) + f64(ground)
    y = (unpack_weight(w4_words, w4_scales, "e4m3").T @ mxq(z, 0, "e4m3")) + f64(b4)[:, None]
    words, scales = planes(y)
    return y, words, scales

@@ -1,0 +1,371 @@
+import math
+from contextlib import ExitStack
+
+import concourse.mybir as mybir
+from concourse.masks import make_identity
+
+K, H, N, T, T3, S, T2 = 1024, 512, 1024, 2048, 1024, 512, 1024
+FLOPS = 2 * (3 * K * H * S + H * N * T2)
+
+F32 = mybir.dt.float32
+BF16 = mybir.dt.bfloat16
+I32 = mybir.dt.int32
+U32 = mybir.dt.uint32
+U16 = mybir.dt.uint16
+U8 = mybir.dt.uint8
+FP8X4 = mybir.dt.float8_e4m3fn_x4
+FP4X4 = mybir.dt.float4_e2m1fn_x4
+ALU = mybir.AluOpType
+ACT = mybir.ActivationFunctionType
+
+P = 128
+PASSES = K // 512
+ROW_TILES = H // P
+HALF = T2 // 2
+TWO_PI = 2.0 * math.pi
+ROUNDER = 1.5 * 2.0**23
+
+
+def tile_list_radar_clutter_map_kernel(
+    tc, tab_words, tab_scales, tab2_words, tab2_scales, offs, offs2, offs3, offs4,
+    w1, w2_words, w2_scales, w3, gain, wg1, wg2, ground, w4_words, w4_scales, b4,
+    out_0, out_1, out_2,
+):
+    nc = tc.nc
+    with ExitStack() as ctx:
+        lists = ctx.enter_context(tc.tile_pool(name="lists", bufs=1))
+        keep = ctx.enter_context(tc.tile_pool(name="keep", bufs=1))
+        ring = ctx.enter_context(tc.tile_pool(name="ring", bufs=2))
+        psum = ctx.enter_context(tc.psum_pool(name="psum", bufs=1))
+
+        def held(name, shape, dtype):
+            return keep.tile(shape, dtype, name=name, align_bytes=64)
+
+        def turn(tag, n, shape, dtype, bufs=2):
+            return ring.tile(shape, dtype, name=f"{tag}{n}", tag=tag, bufs=bufs, align_bytes=64)
+
+        def bank(b, name):
+            return psum.tile([P, 512], F32, name=name, tag=f"bank{b}")
+
+        def stage(slot, name, shape, dtype=F32):
+            return ring.tile(shape, dtype, name=name, tag=f"stage_{slot}", bufs=1, align_bytes=64)
+
+        def load_list(name, src):
+            tile = lists.tile([P, S // 16], U16, name=name)
+            nc.sync.dma_start(tile[:], src)
+            return tile
+
+        def zeroed_bytes(name, shape):
+            tile = held(name, shape, U8)
+            nc.gpsimd.memset(tile[:].bitcast(I32), 0)
+            return tile
+
+        def load_stacked_scales(tile, src, queue=nc.sync):
+            for q in range(4):
+                queue.dma_start(tile[32 * q : 32 * q + 8, :].bitcast(I32), src[:, 4 * q : 4 * q + 4, :].bitcast(I32))
+
+        def load_words(name, src):
+            tile = held(name, [P, src.shape[1]], I32)
+            nc.sync.dma_start(tile[:], src.rearrange("p n i -> p (n i)").bitcast(I32))
+            return tile
+
+        def gather_words(name, window, offsets, slot=None):
+            tile = held(name, [P, S], I32) if slot is None else work(slot, name, I32)
+            nc.vector.tensor_copy(tile[:].bitcast(U32), window[:].bitcast(U32).indirect(offsets[:]))
+            return tile
+
+        def gather_scales(name, window, offsets, slot=None):
+            tile = held(name, [P, S], U8) if slot is None else work(slot, name, U8)
+            nc.vector.tensor_copy(tile[:], window[:].indirect(offsets[:]))
+            return tile
+
+        def load_weight_columns(tile, w, c0, c1):
+            for a in range(PASSES):
+                nc.sync.dma_start(
+                    tile[:, a, :, :], w[512 * a : 512 * (a + 1), c0:c1].rearrange("(p j) c -> p j c", j=4)
+                )
+
+        def quantise_weight(name, rounded):
+            codes = held(name + "_codes", [P, PASSES * P], U32)
+            scales = held(name + "_scales", [P, PASSES * P], U8)
+            nc.vector.quantize_mx(out=codes[:].bitcast(FP8X4), scales=scales[:], in_=rounded[:])
+            return codes, scales
+
+        s2_win = zeroed_bytes("s2_win", [P, T3])
+        s1_win = zeroed_bytes("s1_win", [P, T])
+        w2_sc = zeroed_bytes("w2_sc", [P, PASSES, H])
+        w4_sc_raw = zeroed_bytes("w4_sc_raw", [P, 512])
+        v_sc1 = zeroed_bytes("v_sc1", [P, S])
+        page_b = [held(f"page_b{t}", [P, T2], F32) for t in range(ROW_TILES)]
+        page_a = held("page_a", [P, T2], F32)
+        for page in page_b + [page_a]:
+            nc.vector.memset(page[:], 0.0)
+        ident = held("ident", [P, P], F32)
+        make_identity(nc, ident[:])
+
+        list2 = load_list("list2", offs2)
+        w3_first = [stage(f"first{t}", f"w3_raw{t}", [P, PASSES, 4, P]) for t in range(2)]
+        load_stacked_scales(s2_win, tab2_scales, nc.scalar)
+        tab2_win = [load_words(f"tab2_win{a}", tab2_words[a]) for a in range(PASSES)]
+        load_weight_columns(w3_first[0], w3, 0, P)
+        list1 = load_list("list1", offs)
+        load_stacked_scales(s1_win, tab_scales)
+        list4 = load_list("list4", offs4)
+        gain_t = held("gain_t", [P, ROW_TILES], F32)
+        with nc.allow_non_contiguous_dma(reason="one gain a partition"):
+            nc.sync.dma_start(gain_t[:], gain.rearrange("(t p) -> p t", p=P))
+        wg2_t = held("wg2_t", [P, S], F32)
+        nc.sync.dma_start(wg2_t[:], wg2)
+        load_weight_columns(w3_first[1], w3, P, 2 * P)
+        w3_rest = stage(1, "w3_rest", [P, PASSES, 4, 2 * P])
+        load_weight_columns(w3_rest, w3, 2 * P, 4 * P)
+        tab_win = [load_words("tab_win0", tab_words[0])]
+        w1_raw = [stage(2 + c, f"w1_raw{c}", [P, PASSES, 4, 2 * P]) for c in range(2)]
+        load_weight_columns(w1_raw[0], w1, 0, 2 * P)
+        tab_win.append(load_words("tab_win1", tab_words[1]))
+        w2_w = held("w2_w", [P, PASSES, 2 * H], U8)
+        nc.sync.dma_start(w2_w[:].bitcast(I32), w2_words.rearrange("a p c -> p a c").bitcast(I32))
+        for q in range(4):
+            nc.sync.dma_start(
+                w2_sc[32 * q : 32 * q + 4, :, :].bitcast(I32),
+                w2_scales[:, 4 * q : 4 * q + 4, :].rearrange("a r c -> r a c").bitcast(I32),
+            )
+        wg1_t = held("wg1_t", [P, S], F32)
+        nc.sync.dma_start(wg1_t[:], wg1)
+        list3 = load_list("list3", offs3)
+        load_weight_columns(w1_raw[1], w1, 2 * P, 4 * P)
+
+        v2 = [gather_words("v2_0", tab2_win[0], list2)]
+        v2_sc = gather_scales("v2_sc", s2_win, list2)
+
+        def work(slot, name, dtype=F32):
+            width = S if dtype != BF16 else 2 * S
+            return ring.tile([P, width], dtype, name=name, tag=f"work_{slot}", bufs=1, align_bytes=64)
+
+        def weight_tile(name, raw, slot):
+            rounded = work(slot, name + "_bf", BF16)
+            dst = rounded[:].rearrange("p (a c i j) -> p a c j i", a=PASSES, i=4, j=4)
+            src = raw.rearrange("p a j (c i) -> p a c j i", i=4)
+            for a in range(PASSES):
+                nc.scalar.activation(dst[:, a], src[:, a], ACT.Copy)
+            return quantise_weight(name, rounded)
+
+        def w3_tile(t, slot):
+            raw = w3_first[t][:] if t < 2 else w3_rest[:, :, :, (t - 2) * P : (t - 1) * P]
+            return weight_tile(f"w3_{t}", raw, slot)
+
+        def w1_tile(t, slot):
+            return weight_tile(f"w1_{t}", w1_raw[t // 2][:, :, :, (t % 2) * P : (t % 2 + 1) * P], slot)
+
+        def product(acc, w, moving, moving_scales):
+            codes, scales = w
+            for a in range(PASSES):
+                nc.tensor.matmul_mx(
+                    out=acc[:],
+                    lhsT=codes[:, a * P : (a + 1) * P].bitcast(FP8X4),
+                    lhsT_scale=scales[:, a * P : (a + 1) * P],
+                    rhs=moving[a][:].bitcast(FP8X4),
+                    rhs_scale=moving_scales[4 * a : P, :],
+                    start=(a == 0),
+                    stop=(a == PASSES - 1),
+                )
+
+        def terrain_tanh(t, w3_q):
+            pre = bank(t % 2, f"pre{t}")
+            product(pre, w3_q, v2, v2_sc)
+            th = held(f"th{t}", [P, S], F32)
+            nc.scalar.activation(th[:], pre[:], ACT.Tanh)
+            return th
+
+        def place_terrain(t, th, slot):
+            gained = stage(slot, f"gained{t}", [P, S])
+            nc.scalar.activation(gained[:], wg2_t[:], ACT.Copy, scale=gain_t[:, t : t + 1])
+            nc.vector.tensor_tensor(page_b[t][:].indirect(list4[:]), th[:], gained[:], ALU.mult)
+
+        w3_q = w3_tile(0, "a")
+        v2.append(gather_words("v2_1", tab2_win[1], list2))
+        th = [terrain_tanh(0, w3_q)]
+        v_sc = gather_scales("v_sc", s1_win, list1)
+        for q in range(4):
+            nc.sync.dma_start(v_sc1[32 * q : 32 * q + 4, :].bitcast(I32), v_sc[32 * q + 4 : 32 * q + 8, :].bitcast(I32))
+
+        w4_raw = load_words("w4_raw", w4_words[0])
+        load_stacked_scales(w4_sc_raw, w4_scales[0].rearrange("r (g c) -> g r c", g=2))
+        ground_t = []
+        for t in range(ROW_TILES):
+            tile = held(f"ground{t}", [P, T2], F32)
+            nc.sync.dma_start(tile[:], ground[t * P : (t + 1) * P, :])
+            ground_t.append(tile)
+        b4_t = held("b4_t", [P, 2, 4], F32)
+        nc.sync.dma_start(b4_t[:], b4.rearrange("(g p t) -> p g t", g=2, t=4))
+
+        def gate_products(t, w1_q, slot):
+            phase = bank(2 + t % 2, f"phase{t}")
+            product(phase, w1_q, v, v_sc)
+            amp = bank(4 + t % 2, f"amp{t}")
+            for a in range(PASSES):
+                nc.tensor.matmul_mx(
+                    out=amp[:],
+                    lhsT=w2_w[:, a, 2 * P * t : 2 * P * (t + 1)].bitcast(FP4X4),
+                    lhsT_scale=w2_sc[:, a, P * t : P * (t + 1)],
+                    rhs=v[a][:].bitcast(FP8X4),
+                    rhs_scale=(v_sc if a == 0 else v_sc1)[:],
+                    start=(a == 0),
+                    stop=(a == PASSES - 1),
+                )
+            shifted = turn("shifted", t, [P, S], U32, bufs=1)
+            nc.scalar.activation(shifted[:], phase[:], ACT.Copy, bias=ROUNDER, scale=1.0 / TWO_PI)
+            turns = work(slot, f"turns{t}")
+            nc.scalar.activation(turns[:], shifted[:], ACT.Copy, bias=-ROUNDER, scale=1.0)
+            return phase, amp, turns
+
+        def reduce_phase(t, phase, turns):
+            angle = turn("angle", t, [P, S], F32)
+            nc.vector.scalar_tensor_tensor(angle[:], turns[:], -TWO_PI, phase[:], ALU.mult, ALU.add)
+            return angle
+
+        def take_sine(t, angle):
+            sine = stage(3, "sine0", [P, S]) if t == 0 else turn("sine", t, [P, S], F32)
+            nc.scalar.activation(sine[:], angle[:], ACT.Sin)
+            return sine
+
+        def weigh_amp(t, amp, slot):
+            weighed = work(slot, f"weighed{t}")
+            nc.vector.tensor_tensor(weighed[:], amp[:], wg1_t[:], ALU.mult)
+            return weighed
+
+        z_turned = [held(f"z_turned{h}", [P, 4 * H], BF16) for h in range(2)]
+
+        def turn_ground(t):
+            banks = []
+            for h in range(2):
+                acc = bank((6 if t % 2 == 0 else 0) + h, f"zt{t}_{h}")
+                for b in range(4):
+                    cols = slice(h * HALF + b * P, h * HALF + (b + 1) * P)
+                    nc.tensor.matmul(
+                        acc[:, b * P : (b + 1) * P], ground_t[t][:, cols], ident[:],
+                        start=(b == 0), stop=False, is_transpose=True,
+                    )
+                banks.append(acc)
+            return banks
+
+        largers = []
+
+        def combine(t, banks):
+            for h in range(2):
+                larger = turn("larger", 2 * t + h, [P, HALF], F32, bufs=4)
+                cols = slice(h * HALF, (h + 1) * HALF)
+                nc.vector.tensor_tensor(larger[:], page_a[:, cols], page_b[t][:, cols], ALU.max)
+                largers.append(larger)
+                acc = banks[h]
+                for b in range(4):
+                    nc.tensor.matmul(
+                        acc[:, b * P : (b + 1) * P], larger[:, b * P : (b + 1) * P], ident[:],
+                        start=False, stop=(b == 3), is_transpose=True,
+                    )
+                nc.scalar.copy(
+                    z_turned[h][:].rearrange("p (b u q e) -> p b u q e", b=4, u=2, e=2)[:, :, :, 32 * t : 32 * (t + 1), :],
+                    acc[:].rearrange("p (b q u e) -> p b u q e", b=4, u=2, e=2),
+                )
+
+        w3_q = w3_tile(1, "b")
+        place_terrain(0, th[0], "first1")
+        th.append(terrain_tanh(1, w3_q))
+        th.append(terrain_tanh(2, w3_tile(2, "a")))
+        v = [gather_words("v_0", tab_win[0], list1)]
+        th.append(terrain_tanh(3, w3_tile(3, "b")))
+        place_terrain(1, th[1], 1)
+        w1_q = [w1_tile(0, "a")]
+        v.append(gather_words("v_1", tab_win[1], list1))
+        w1_q.append(w1_tile(1, "b"))
+        place_terrain(2, th[2], 2)
+        place_terrain(3, th[3], "first0")
+        turn_slot = ["e", "f", "g", "h"]
+        prods = [gate_products(t, w1_q[t], turn_slot[t]) for t in range(2)]
+        angles = [reduce_phase(0, prods[0][0], prods[0][2])]
+        w1_q.append(w1_tile(2, "a"))
+        w1_q.append(w1_tile(3, "b"))
+        w4_w = held("w4_w", [P, N], I32)
+        w4_sc = held("w4_sc", [P, 512], U8)
+        for t in range(ROW_TILES):
+            sine = take_sine(t, angles[t])
+            if t + 1 < ROW_TILES:
+                angles.append(reduce_phase(t + 1, prods[t + 1][0], prods[t + 1][2]))
+            weighed = weigh_amp(t, prods[t][1], turn_slot[(t + 1) % ROW_TILES])
+            banks = turn_ground(t)
+            if t + 2 < ROW_TILES:
+                prods.append(gate_products(t + 2, w1_q[t + 2], turn_slot[t + 2]))
+            if t == ROW_TILES - 1:
+                nc.vector.tensor_copy(
+                    w4_w[:].rearrange("p (g t q) -> p g t q", g=2, t=4),
+                    w4_raw[:].rearrange("p (g q t) -> p g t q", g=2, t=4),
+                )
+                nc.vector.tensor_copy(
+                    w4_sc[:].rearrange("p (t q) -> p t q", t=4),
+                    w4_sc_raw[:].rearrange("p (q t) -> p t q", t=4),
+                )
+            nc.vector.tensor_tensor(page_a[:].indirect(list3[:]), sine[:], weighed[:], ALU.mult)
+            combine(t, banks)
+
+        def quantise_z(h):
+            words = z_turned[h][:].bitcast(F32)
+            z_in = held(f"z_in{h}", [P, 4 * HALF], BF16)
+            for d in range(2):
+                acc = bank(2 + 2 * h + d, f"zback{h}_{d}")
+                for s in range(4):
+                    nc.tensor.transpose(
+                        acc[:, s * P : (s + 1) * P], words[:, (4 * d + s) * P : (4 * d + s + 1) * P], ident[:]
+                    )
+                dst = z_in[:].bitcast(F32)[:, 512 * d : 512 * (d + 1)].rearrange("p (b m u) -> p b m u", b=2, u=2)
+                src = acc[:].rearrange("p (b u m) -> p b m u", b=2, u=2)
+                if d == 0:
+                    nc.vector.tensor_copy(dst, src)
+                else:
+                    nc.scalar.copy(dst, src)
+            codes = held(f"z_codes{h}", [P, HALF], U32)
+            scales = held(f"z_scales{h}", [P, HALF], U8)
+            nc.vector.quantize_mx(out=codes[:].bitcast(FP8X4), scales=scales[:], in_=z_in[:])
+            return codes, scales
+
+        z_q = [quantise_z(h) for h in range(2)]
+
+        out_rows = out_0.rearrange("(g p t) m -> g p t m", g=2, t=4)
+        for h in range(2):
+            cols = slice(h * HALF, (h + 1) * HALF)
+            y_scales = held(f"y_scales{h}", [P, 2, HALF], U8)
+            for g in range(2):
+                unit = 2 * h + g
+                y = stage(unit, f"y{unit}", [P, 4, HALF])
+                for t in range(4):
+                    acc = bank((6 + 4 * unit + t) % 8, f"y{unit}_{t}")
+                    nc.tensor.matmul_mx(
+                        out=acc[:],
+                        lhsT=w4_w[:, (4 * g + t) * P : (4 * g + t + 1) * P].bitcast(FP8X4),
+                        lhsT_scale=w4_sc[4 * g : P, t * P : (t + 1) * P],
+                        rhs=z_q[h][0][:].bitcast(FP8X4),
+                        rhs_scale=z_q[h][1][:],
+                        start=True,
+                        stop=True,
+                    )
+                    bias = b4_t[:, g, t : t + 1]
+                    if unit == 0 and t % 2 == 1:
+                        nc.vector.tensor_scalar(y[:, t, :], acc[:], bias, None, ALU.add)
+                    else:
+                        nc.scalar.activation(y[:, t, :], acc[:], ACT.Identity, bias=bias)
+                    if unit == 0:
+                        nc.sync.dma_start(out_rows[g][:, t, cols], y[:, t, :])
+                    elif t % 2 == 1:
+                        nc.sync.dma_start(out_rows[g][:, t - 1 : t + 1, cols], y[:, t - 1 : t + 1, :])
+                y_bf = turn("y_bf", unit, [P, 4 * HALF], BF16)
+                nc.vector.tensor_copy(
+                    y_bf[:].rearrange("p (c i t) -> p c t i", i=4, t=4),
+                    y[:].rearrange("p t (c i) -> p c t i", i=4),
+                )
+                y_codes = held(f"y_codes{unit}", [P, HALF], I32)
+                nc.vector.quantize_mx(out=y_codes[:].bitcast(FP8X4), scales=y_scales[:, g, :], in_=y_bf[:])
+                nc.sync.dma_start(out_1[g][:, cols, :].rearrange("p m i -> p (m i)").bitcast(I32), y_codes[:])
+            for q in range(4):
+                nc.sync.dma_start(
+                    out_2[:, 4 * q : 4 * q + 4, cols].rearrange("g r c -> r g c").bitcast(I32),
+                    y_scales[32 * q : 32 * q + 4, :, :].bitcast(I32),
+                )

@@ -57,15 +57,16 @@ def tile_list_radar_clutter_map_kernel(
 
         def zeroed_bytes(name, shape):
             tile = held(name, shape, U8)
-            nc.gpsimd.memset(tile[:].bitcast(I32), 0)
+            nc.vector.memset(tile[:].bitcast(I32), 0)
             return tile
 
         def load_stacked_scales(tile, src, queue=nc.sync):
             for q in range(4):
                 queue.dma_start(tile[32 * q : 32 * q + 8, :].bitcast(I32), src[:, 4 * q : 4 * q + 4, :].bitcast(I32))
 
-        def load_words(name, src):
-            tile = held(name, [P, src.shape[1]], I32)
+        def load_words(name, src, slot=None):
+            shape = [P, src.shape[1]]
+            tile = held(name, shape, I32) if slot is None else stage(slot, name, shape, I32)
             nc.sync.dma_start(tile[:], src.rearrange("p n i -> p (n i)").bitcast(I32))
             return tile
 
@@ -75,7 +76,7 @@ def tile_list_radar_clutter_map_kernel(
             return tile
 
         def gather_scales(name, window, offsets, slot=None):
-            tile = held(name, [P, S], U8) if slot is None else work(slot, name, U8)
+            tile = held(name, [P, S], U8) if slot is None else stage(slot, name, [P, S], U8)
             nc.vector.tensor_copy(tile[:], window[:].indirect(offsets[:]))
             return tile
 
@@ -93,36 +94,35 @@ def tile_list_radar_clutter_map_kernel(
 
         s2_win = zeroed_bytes("s2_win", [P, T3])
         s1_win = zeroed_bytes("s1_win", [P, T])
-        w2_sc = zeroed_bytes("w2_sc", [P, PASSES, H])
-        w4_sc_raw = zeroed_bytes("w4_sc_raw", [P, 512])
-        v_sc1 = zeroed_bytes("v_sc1", [P, S])
         page_b = [held(f"page_b{t}", [P, T2], F32) for t in range(ROW_TILES)]
         page_a = held("page_a", [P, T2], F32)
         for page in page_b + [page_a]:
-            nc.vector.memset(page[:], 0.0)
+            nc.vector.memset(page[:].bitcast(I32), 0)
+        w2_sc = zeroed_bytes("w2_sc", [P, PASSES, H])
+        w4_sc_raw = zeroed_bytes("w4_sc_raw", [P, 512])
+        v_sc1 = zeroed_bytes("v_sc1", [P, S])
         ident = held("ident", [P, P], F32)
         make_identity(nc, ident[:])
 
         list2 = load_list("list2", offs2)
-        w3_first = [stage(f"first{t}", f"w3_raw{t}", [P, PASSES, 4, P]) for t in range(2)]
-        load_stacked_scales(s2_win, tab2_scales, nc.scalar)
-        tab2_win = [load_words(f"tab2_win{a}", tab2_words[a]) for a in range(PASSES)]
-        load_weight_columns(w3_first[0], w3, 0, P)
-        list1 = load_list("list1", offs)
-        load_stacked_scales(s1_win, tab_scales)
+        load_stacked_scales(s2_win, tab2_scales)
+        w3_first = stage("w3_0", "w3_first", [P, PASSES, 4, P])
+        tab2_win = [load_words("tab2_win0", tab2_words[0])]
+        load_weight_columns(w3_first, w3, 0, P)
+        tab2_win.append(load_words("tab2_win1", tab2_words[1]))
         list4 = load_list("list4", offs4)
         gain_t = held("gain_t", [P, ROW_TILES], F32)
         with nc.allow_non_contiguous_dma(reason="one gain a partition"):
             nc.sync.dma_start(gain_t[:], gain.rearrange("(t p) -> p t", p=P))
         wg2_t = held("wg2_t", [P, S], F32)
         nc.sync.dma_start(wg2_t[:], wg2)
-        load_weight_columns(w3_first[1], w3, P, 2 * P)
-        w3_rest = stage(1, "w3_rest", [P, PASSES, 4, 2 * P])
-        load_weight_columns(w3_rest, w3, 2 * P, 4 * P)
-        tab_win = [load_words("tab_win0", tab_words[0])]
+        list1 = load_list("list1", offs)
+        w3_rest = stage(1, "w3_rest", [P, PASSES, 4, 3 * P])
+        load_weight_columns(w3_rest, w3, P, 4 * P)
+        load_stacked_scales(s1_win, tab_scales)
+        tab_win = [load_words(f"tab_win{a}", tab_words[a]) for a in range(PASSES)]
         w1_raw = [stage(2 + c, f"w1_raw{c}", [P, PASSES, 4, 2 * P]) for c in range(2)]
         load_weight_columns(w1_raw[0], w1, 0, 2 * P)
-        tab_win.append(load_words("tab_win1", tab_words[1]))
         w2_w = held("w2_w", [P, PASSES, 2 * H], U8)
         nc.sync.dma_start(w2_w[:].bitcast(I32), w2_words.rearrange("a p c -> p a c").bitcast(I32))
         for q in range(4):
@@ -146,16 +146,20 @@ def tile_list_radar_clutter_map_kernel(
             rounded = work(slot, name + "_bf", BF16)
             dst = rounded[:].rearrange("p (a c i j) -> p a c j i", a=PASSES, i=4, j=4)
             src = raw.rearrange("p a j (c i) -> p a c j i", i=4)
-            for a in range(PASSES):
-                nc.scalar.activation(dst[:, a], src[:, a], ACT.Copy)
+            if name == "w3_0":
+                for a in range(PASSES):
+                    nc.scalar.activation(dst[:, a], src[:, a], ACT.Copy)
+            else:
+                nc.scalar.copy(dst, src)
             return quantise_weight(name, rounded)
 
         def w3_tile(t, slot):
-            raw = w3_first[t][:] if t < 2 else w3_rest[:, :, :, (t - 2) * P : (t - 1) * P]
+            raw = w3_first[:] if t == 0 else w3_rest[:, :, :, (t - 1) * P : t * P]
             return weight_tile(f"w3_{t}", raw, slot)
 
         def w1_tile(t, slot):
-            return weight_tile(f"w1_{t}", w1_raw[t // 2][:, :, :, (t % 2) * P : (t % 2 + 1) * P], slot)
+            raw = w1_raw[t // 2][:, :, :, (t % 2) * P : (t % 2 + 1) * P]
+            return weight_tile(f"w1_{t}", raw, slot)
 
         def product(acc, w, moving, moving_scales):
             codes, scales = w
@@ -182,26 +186,20 @@ def tile_list_radar_clutter_map_kernel(
             nc.scalar.activation(gained[:], wg2_t[:], ACT.Copy, scale=gain_t[:, t : t + 1])
             nc.vector.tensor_tensor(page_b[t][:].indirect(list4[:]), th[:], gained[:], ALU.mult)
 
-        w3_q = w3_tile(0, "a")
-        v2.append(gather_words("v2_1", tab2_win[1], list2))
+        w3_q = w3_tile(0, "k")
+        v2.append(gather_words("v2_1", tab2_win[1], list2, "k"))
         th = [terrain_tanh(0, w3_q)]
-        v_sc = gather_scales("v_sc", s1_win, list1)
-        for q in range(4):
-            nc.sync.dma_start(v_sc1[32 * q : 32 * q + 4, :].bitcast(I32), v_sc[32 * q + 4 : 32 * q + 8, :].bitcast(I32))
-
-        w4_raw = load_words("w4_raw", w4_words[0])
-        load_stacked_scales(w4_sc_raw, w4_scales[0].rearrange("r (g c) -> g r c", g=2))
         ground_t = []
         for t in range(ROW_TILES):
             tile = held(f"ground{t}", [P, T2], F32)
             nc.sync.dma_start(tile[:], ground[t * P : (t + 1) * P, :])
             ground_t.append(tile)
+        w4_raw = load_words("w4_raw", w4_words[0])
+        load_stacked_scales(w4_sc_raw, w4_scales[0].rearrange("r (g c) -> g r c", g=2))
         b4_t = held("b4_t", [P, 2, 4], F32)
         nc.sync.dma_start(b4_t[:], b4.rearrange("(g p t) -> p g t", g=2, t=4))
 
-        def gate_products(t, w1_q, slot):
-            phase = bank(2 + t % 2, f"phase{t}")
-            product(phase, w1_q, v, v_sc)
+        def gate_amplitude(t):
             amp = bank(4 + t % 2, f"amp{t}")
             for a in range(PASSES):
                 nc.tensor.matmul_mx(
@@ -213,11 +211,16 @@ def tile_list_radar_clutter_map_kernel(
                     start=(a == 0),
                     stop=(a == PASSES - 1),
                 )
+            return amp
+
+        def gate_phase(t, w1_q, slot):
+            phase = bank(2 + t % 2, f"phase{t}")
+            product(phase, w1_q, v, v_sc)
             shifted = turn("shifted", t, [P, S], U32, bufs=1)
             nc.scalar.activation(shifted[:], phase[:], ACT.Copy, bias=ROUNDER, scale=1.0 / TWO_PI)
             turns = work(slot, f"turns{t}")
             nc.scalar.activation(turns[:], shifted[:], ACT.Copy, bias=-ROUNDER, scale=1.0)
-            return phase, amp, turns
+            return phase, turns
 
         def reduce_phase(t, phase, turns):
             angle = turn("angle", t, [P, S], F32)
@@ -225,7 +228,7 @@ def tile_list_radar_clutter_map_kernel(
             return angle
 
         def take_sine(t, angle):
-            sine = stage(3, "sine0", [P, S]) if t == 0 else turn("sine", t, [P, S], F32)
+            sine = stage(3, "sine0", [P, S]) if t == 0 else work(f"s{t % 2}", f"sine{t}")
             nc.scalar.activation(sine[:], angle[:], ACT.Sin)
             return sine
 
@@ -234,7 +237,7 @@ def tile_list_radar_clutter_map_kernel(
             nc.vector.tensor_tensor(weighed[:], amp[:], wg1_t[:], ALU.mult)
             return weighed
 
-        z_turned = [held(f"z_turned{h}", [P, 4 * H], BF16) for h in range(2)]
+        z_turned = [held(f"z_turned{h}", [P, 4 * HALF], BF16) for h in range(2)]
 
         def turn_ground(t):
             banks = []
@@ -249,18 +252,19 @@ def tile_list_radar_clutter_map_kernel(
                 banks.append(acc)
             return banks
 
-        largers = []
-
         def combine(t, banks):
+            larger = turn("larger", t, [P, T2], F32)
+            last = t == ROW_TILES - 1
+            if not last:
+                nc.vector.tensor_tensor(larger[:], page_a[:], page_b[t][:], ALU.max)
             for h in range(2):
-                larger = turn("larger", 2 * t + h, [P, HALF], F32, bufs=4)
                 cols = slice(h * HALF, (h + 1) * HALF)
-                nc.vector.tensor_tensor(larger[:], page_a[:, cols], page_b[t][:, cols], ALU.max)
-                largers.append(larger)
+                if last:
+                    nc.vector.tensor_tensor(larger[:, cols], page_a[:, cols], page_b[t][:, cols], ALU.max)
                 acc = banks[h]
                 for b in range(4):
                     nc.tensor.matmul(
-                        acc[:, b * P : (b + 1) * P], larger[:, b * P : (b + 1) * P], ident[:],
+                        acc[:, b * P : (b + 1) * P], larger[:, h * HALF + b * P : h * HALF + (b + 1) * P], ident[:],
                         start=False, stop=(b == 3), is_transpose=True,
                     )
                 nc.scalar.copy(
@@ -268,44 +272,46 @@ def tile_list_radar_clutter_map_kernel(
                     acc[:].rearrange("p (b q u e) -> p b u q e", b=4, u=2, e=2),
                 )
 
-        w3_q = w3_tile(1, "b")
-        place_terrain(0, th[0], "first1")
-        th.append(terrain_tanh(1, w3_q))
-        th.append(terrain_tanh(2, w3_tile(2, "a")))
+        place_terrain(0, th[0], "w3_0")
+        v_sc = gather_scales("v_sc", s1_win, list1, "w3_0")
+        nc.sync.dma_start(v_sc1[0:100, :].bitcast(I32), v_sc[4:104, :].bitcast(I32))
+        th.append(terrain_tanh(1, w3_tile(1, "b")))
         v = [gather_words("v_0", tab_win[0], list1)]
+        th.append(terrain_tanh(2, w3_tile(2, "a")))
         th.append(terrain_tanh(3, w3_tile(3, "b")))
         place_terrain(1, th[1], 1)
-        w1_q = [w1_tile(0, "a")]
         v.append(gather_words("v_1", tab_win[1], list1))
-        w1_q.append(w1_tile(1, "b"))
+        w1_q = [w1_tile(0, "a"), w1_tile(1, "b")]
         place_terrain(2, th[2], 2)
-        place_terrain(3, th[3], "first0")
         turn_slot = ["e", "f", "g", "h"]
-        prods = [gate_products(t, w1_q[t], turn_slot[t]) for t in range(2)]
-        angles = [reduce_phase(0, prods[0][0], prods[0][2])]
+        phases = [gate_phase(t, w1_q[t], turn_slot[t]) for t in range(2)]
+        amps = [gate_amplitude(t) for t in range(2)]
+        angles = [reduce_phase(0, *phases[0])]
+        place_terrain(3, th[3], 2)
         w1_q.append(w1_tile(2, "a"))
         w1_q.append(w1_tile(3, "b"))
-        w4_w = held("w4_w", [P, N], I32)
-        w4_sc = held("w4_sc", [P, 512], U8)
         for t in range(ROW_TILES):
             sine = take_sine(t, angles[t])
             if t + 1 < ROW_TILES:
-                angles.append(reduce_phase(t + 1, prods[t + 1][0], prods[t + 1][2]))
-            weighed = weigh_amp(t, prods[t][1], turn_slot[(t + 1) % ROW_TILES])
+                angles.append(reduce_phase(t + 1, *phases[t + 1]))
+            weighed = weigh_amp(t, amps[t], turn_slot[(t + 1) % ROW_TILES])
             banks = turn_ground(t)
             if t + 2 < ROW_TILES:
-                prods.append(gate_products(t + 2, w1_q[t + 2], turn_slot[t + 2]))
-            if t == ROW_TILES - 1:
-                nc.vector.tensor_copy(
-                    w4_w[:].rearrange("p (g t q) -> p g t q", g=2, t=4),
-                    w4_raw[:].rearrange("p (g q t) -> p g t q", g=2, t=4),
-                )
-                nc.vector.tensor_copy(
-                    w4_sc[:].rearrange("p (t q) -> p t q", t=4),
-                    w4_sc_raw[:].rearrange("p (q t) -> p t q", t=4),
-                )
+                phases.append(gate_phase(t + 2, w1_q[t + 2], turn_slot[t + 2]))
+                amps.append(gate_amplitude(t + 2))
             nc.vector.tensor_tensor(page_a[:].indirect(list3[:]), sine[:], weighed[:], ALU.mult)
             combine(t, banks)
+
+        w4_w = ring.tile([P, N], I32, name="w4_w", tag="work_e", bufs=1, align_bytes=64)
+        nc.vector.tensor_copy(
+            w4_w[:].rearrange("p (g t q) -> p g t q", g=2, t=4),
+            w4_raw[:].rearrange("p (g q t) -> p g t q", g=2, t=4),
+        )
+        w4_sc = ring.tile([P, 512], U8, name="w4_sc", tag="work_s1", bufs=1, align_bytes=64)
+        nc.vector.tensor_copy(
+            w4_sc[:].rearrange("p (t q) -> p t q", t=4),
+            w4_sc_raw[:].rearrange("p (q t) -> p t q", t=4),
+        )
 
         def quantise_z(h):
             words = z_turned[h][:].bitcast(F32)
@@ -330,9 +336,9 @@ def tile_list_radar_clutter_map_kernel(
         z_q = [quantise_z(h) for h in range(2)]
 
         out_rows = out_0.rearrange("(g p t) m -> g p t m", g=2, t=4)
+        y_scales = held("y_scales", [P, 2, T2], U8)
         for h in range(2):
             cols = slice(h * HALF, (h + 1) * HALF)
-            y_scales = held(f"y_scales{h}", [P, 2, HALF], U8)
             for g in range(2):
                 unit = 2 * h + g
                 y = stage(unit, f"y{unit}", [P, 4, HALF])
@@ -362,10 +368,10 @@ def tile_list_radar_clutter_map_kernel(
                     y[:].rearrange("p t (c i) -> p c t i", i=4),
                 )
                 y_codes = held(f"y_codes{unit}", [P, HALF], I32)
-                nc.vector.quantize_mx(out=y_codes[:].bitcast(FP8X4), scales=y_scales[:, g, :], in_=y_bf[:])
+                nc.vector.quantize_mx(out=y_codes[:].bitcast(FP8X4), scales=y_scales[:, g, cols], in_=y_bf[:])
                 nc.sync.dma_start(out_1[g][:, cols, :].rearrange("p m i -> p (m i)").bitcast(I32), y_codes[:])
-            for q in range(4):
-                nc.sync.dma_start(
-                    out_2[:, 4 * q : 4 * q + 4, cols].rearrange("g r c -> r g c").bitcast(I32),
-                    y_scales[32 * q : 32 * q + 4, :, :].bitcast(I32),
-                )
+        for q in range(4):
+            nc.sync.dma_start(
+                out_2[:, 4 * q : 4 * q + 4, :].rearrange("g r c -> r g c").bitcast(I32),
+                y_scales[32 * q : 32 * q + 4, :, :].bitcast(I32),
+            )

@@ -64,14 +64,13 @@ def tile_list_radar_clutter_map_kernel(
             for q in range(4):
                 queue.dma_start(tile[32 * q : 32 * q + 8, :].bitcast(I32), src[:, 4 * q : 4 * q + 4, :].bitcast(I32))
 
-        def load_words(name, src, slot=None):
-            shape = [P, src.shape[1]]
-            tile = held(name, shape, I32) if slot is None else stage(slot, name, shape, I32)
+        def load_words(name, src):
+            tile = held(name, [P, src.shape[1]], I32)
             nc.sync.dma_start(tile[:], src.rearrange("p n i -> p (n i)").bitcast(I32))
             return tile
 
         def gather_words(name, window, offsets, slot=None):
-            tile = held(name, [P, S], I32) if slot is None else work(slot, name, I32)
+            tile = held(name, [P, S], I32) if slot is None else stage(slot, name, [P, S], I32)
             nc.vector.tensor_copy(tile[:].bitcast(U32), window[:].bitcast(U32).indirect(offsets[:]))
             return tile
 
@@ -94,9 +93,8 @@ def tile_list_radar_clutter_map_kernel(
 
         s2_win = zeroed_bytes("s2_win", [P, T3])
         s1_win = zeroed_bytes("s1_win", [P, T])
-        page_b = [held(f"page_b{t}", [P, T2], F32) for t in range(ROW_TILES)]
-        page_a = held("page_a", [P, T2], F32)
-        for page in page_b + [page_a]:
+        page_b = [held(f"page_b{t}", [P, T2], F32) for t in range(ROW_TILES - 1)]
+        for page in page_b:
             nc.vector.memset(page[:].bitcast(I32), 0)
         w2_sc = zeroed_bytes("w2_sc", [P, PASSES, H])
         w4_sc_raw = zeroed_bytes("w4_sc_raw", [P, 512])
@@ -105,24 +103,26 @@ def tile_list_radar_clutter_map_kernel(
         make_identity(nc, ident[:])
 
         list2 = load_list("list2", offs2)
-        load_stacked_scales(s2_win, tab2_scales)
-        w3_first = stage("w3_0", "w3_first", [P, PASSES, 4, P])
-        tab2_win = [load_words("tab2_win0", tab2_words[0])]
-        load_weight_columns(w3_first, w3, 0, P)
-        tab2_win.append(load_words("tab2_win1", tab2_words[1]))
+        list1 = load_list("list1", offs)
         list4 = load_list("list4", offs4)
+        list3 = load_list("list3", offs3)
+        tab2_win = [load_words(f"tab2_win{a}", tab2_words[a]) for a in range(PASSES)]
+        w3_first = stage("w3_first", "w3_first", [P, PASSES, 4, P])
+        load_weight_columns(w3_first, w3, 0, P)
+        load_stacked_scales(s2_win, tab2_scales)
+        wg2_t = stage("wg2", "wg2_t", [P, S])
+        nc.sync.dma_start(wg2_t[:], wg2)
         gain_t = held("gain_t", [P, ROW_TILES], F32)
         with nc.allow_non_contiguous_dma(reason="one gain a partition"):
             nc.sync.dma_start(gain_t[:], gain.rearrange("(t p) -> p t", p=P))
-        wg2_t = held("wg2_t", [P, S], F32)
-        nc.sync.dma_start(wg2_t[:], wg2)
-        list1 = load_list("list1", offs)
         w3_rest = stage(1, "w3_rest", [P, PASSES, 4, 3 * P])
         load_weight_columns(w3_rest, w3, P, 4 * P)
         load_stacked_scales(s1_win, tab_scales)
-        tab_win = [load_words(f"tab_win{a}", tab_words[a]) for a in range(PASSES)]
+        tab_win = [load_words("tab_win0", tab_words[0])]
         w1_raw = [stage(2 + c, f"w1_raw{c}", [P, PASSES, 4, 2 * P]) for c in range(2)]
         load_weight_columns(w1_raw[0], w1, 0, 2 * P)
+        tab_win.append(load_words("tab_win1", tab_words[1]))
+        load_weight_columns(w1_raw[1], w1, 2 * P, 4 * P)
         w2_w = held("w2_w", [P, PASSES, 2 * H], U8)
         nc.sync.dma_start(w2_w[:].bitcast(I32), w2_words.rearrange("a p c -> p a c").bitcast(I32))
         for q in range(4):
@@ -130,20 +130,12 @@ def tile_list_radar_clutter_map_kernel(
                 w2_sc[32 * q : 32 * q + 4, :, :].bitcast(I32),
                 w2_scales[:, 4 * q : 4 * q + 4, :].rearrange("a r c -> r a c").bitcast(I32),
             )
-        wg1_t = held("wg1_t", [P, S], F32)
-        nc.sync.dma_start(wg1_t[:], wg1)
-        list3 = load_list("list3", offs3)
-        load_weight_columns(w1_raw[1], w1, 2 * P, 4 * P)
 
-        v2 = [gather_words("v2_0", tab2_win[0], list2)]
+        v2 = [gather_words(f"v2_{a}", tab2_win[a], list2) for a in range(PASSES)]
         v2_sc = gather_scales("v2_sc", s2_win, list2)
 
-        def work(slot, name, dtype=F32):
-            width = S if dtype != BF16 else 2 * S
-            return ring.tile([P, width], dtype, name=name, tag=f"work_{slot}", bufs=1, align_bytes=64)
-
         def weight_tile(name, raw, slot):
-            rounded = work(slot, name + "_bf", BF16)
+            rounded = stage(f"rounded{slot}", name + "_bf", [P, 2 * S], BF16)
             dst = rounded[:].rearrange("p (a c i j) -> p a c j i", a=PASSES, i=4, j=4)
             src = raw.rearrange("p a j (c i) -> p a c j i", i=4)
             if name == "w3_0":
@@ -153,13 +145,13 @@ def tile_list_radar_clutter_map_kernel(
                 nc.scalar.copy(dst, src)
             return quantise_weight(name, rounded)
 
-        def w3_tile(t, slot):
+        def w3_tile(t):
             raw = w3_first[:] if t == 0 else w3_rest[:, :, :, (t - 1) * P : t * P]
-            return weight_tile(f"w3_{t}", raw, slot)
+            return weight_tile(f"w3_{t}", raw, t)
 
-        def w1_tile(t, slot):
+        def w1_tile(t):
             raw = w1_raw[t // 2][:, :, :, (t % 2) * P : (t % 2 + 1) * P]
-            return weight_tile(f"w1_{t}", raw, slot)
+            return weight_tile(f"w1_{t}", raw, (1, 4)[t % 2])
 
         def product(acc, w, moving, moving_scales):
             codes, scales = w
@@ -177,27 +169,19 @@ def tile_list_radar_clutter_map_kernel(
         def terrain_tanh(t, w3_q):
             pre = bank(t % 2, f"pre{t}")
             product(pre, w3_q, v2, v2_sc)
-            th = held(f"th{t}", [P, S], F32)
+            th = stage(f"th{t}", f"th{t}", [P, S])
             nc.scalar.activation(th[:], pre[:], ACT.Tanh)
             return th
 
-        def place_terrain(t, th, slot):
-            gained = stage(slot, f"gained{t}", [P, S])
-            nc.scalar.activation(gained[:], wg2_t[:], ACT.Copy, scale=gain_t[:, t : t + 1])
-            nc.vector.tensor_tensor(page_b[t][:].indirect(list4[:]), th[:], gained[:], ALU.mult)
+        def place_terrain(t, th, gained):
+            nc.scalar.activation(gained, wg2_t[:], ACT.Copy, scale=gain_t[:, t : t + 1])
+            nc.vector.tensor_tensor(page_b[t][:].indirect(list4[:]), th[:], gained, ALU.mult)
 
-        w3_q = w3_tile(0, "k")
-        v2.append(gather_words("v2_1", tab2_win[1], list2, "k"))
-        th = [terrain_tanh(0, w3_q)]
-        ground_t = []
-        for t in range(ROW_TILES):
-            tile = held(f"ground{t}", [P, T2], F32)
-            nc.sync.dma_start(tile[:], ground[t * P : (t + 1) * P, :])
-            ground_t.append(tile)
-        w4_raw = load_words("w4_raw", w4_words[0])
-        load_stacked_scales(w4_sc_raw, w4_scales[0].rearrange("r (g c) -> g r c", g=2))
-        b4_t = held("b4_t", [P, 2, 4], F32)
-        nc.sync.dma_start(b4_t[:], b4.rearrange("(g p t) -> p g t", g=2, t=4))
+        th = [terrain_tanh(0, w3_tile(0))]
+        page_b.append(stage("rounded0", "page_b3", [P, T2]))
+        page_a = stage("w3_first", "page_a", [P, T2])
+        for page in (page_b[3], page_a):
+            nc.vector.memset(page[:].bitcast(I32), 0)
 
         def gate_amplitude(t):
             amp = bank(4 + t % 2, f"amp{t}")
@@ -213,12 +197,12 @@ def tile_list_radar_clutter_map_kernel(
                 )
             return amp
 
-        def gate_phase(t, w1_q, slot):
+        def gate_phase(t, w1_q):
             phase = bank(2 + t % 2, f"phase{t}")
             product(phase, w1_q, v, v_sc)
             shifted = turn("shifted", t, [P, S], U32, bufs=1)
             nc.scalar.activation(shifted[:], phase[:], ACT.Copy, bias=ROUNDER, scale=1.0 / TWO_PI)
-            turns = work(slot, f"turns{t}")
+            turns = turn("turns", t, [P, S], F32)
             nc.scalar.activation(turns[:], shifted[:], ACT.Copy, bias=-ROUNDER, scale=1.0)
             return phase, turns
 
@@ -228,12 +212,12 @@ def tile_list_radar_clutter_map_kernel(
             return angle
 
         def take_sine(t, angle):
-            sine = stage(3, "sine0", [P, S]) if t == 0 else work(f"s{t % 2}", f"sine{t}")
+            sine = stage("wg2" if t == 0 else f"sine{t % 2}", f"sine{t}", [P, S])
             nc.scalar.activation(sine[:], angle[:], ACT.Sin)
             return sine
 
-        def weigh_amp(t, amp, slot):
-            weighed = work(slot, f"weighed{t}")
+        def weigh_amp(t, amp):
+            weighed = stage((2, "th2")[t % 2], f"weighed{t}", [P, S])
             nc.vector.tensor_tensor(weighed[:], amp[:], wg1_t[:], ALU.mult)
             return weighed
 
@@ -272,42 +256,55 @@ def tile_list_radar_clutter_map_kernel(
                     acc[:].rearrange("p (b q u e) -> p b u q e", b=4, u=2, e=2),
                 )
 
-        place_terrain(0, th[0], "w3_0")
-        v_sc = gather_scales("v_sc", s1_win, list1, "w3_0")
+        place_terrain(0, th[0], held("gained0", [P, S], F32)[:])
+        for t in range(1, ROW_TILES):
+            th.append(terrain_tanh(t, w3_tile(t)))
+        v_sc = gather_scales("v_sc", s1_win, list1, "rounded2")
         nc.sync.dma_start(v_sc1[0:100, :].bitcast(I32), v_sc[4:104, :].bitcast(I32))
-        th.append(terrain_tanh(1, w3_tile(1, "b")))
-        v = [gather_words("v_0", tab_win[0], list1)]
-        th.append(terrain_tanh(2, w3_tile(2, "a")))
-        th.append(terrain_tanh(3, w3_tile(3, "b")))
-        place_terrain(1, th[1], 1)
-        v.append(gather_words("v_1", tab_win[1], list1))
-        w1_q = [w1_tile(0, "a"), w1_tile(1, "b")]
-        place_terrain(2, th[2], 2)
-        turn_slot = ["e", "f", "g", "h"]
-        phases = [gate_phase(t, w1_q[t], turn_slot[t]) for t in range(2)]
-        amps = [gate_amplitude(t) for t in range(2)]
-        angles = [reduce_phase(0, *phases[0])]
-        place_terrain(3, th[3], 2)
-        w1_q.append(w1_tile(2, "a"))
-        w1_q.append(w1_tile(3, "b"))
+        wg1_t = held("wg1_t", [P, S], F32)
+        nc.sync.dma_start(wg1_t[:], wg1)
+        ground_t = []
         for t in range(ROW_TILES):
-            sine = take_sine(t, angles[t])
-            if t + 1 < ROW_TILES:
-                angles.append(reduce_phase(t + 1, *phases[t + 1]))
-            weighed = weigh_amp(t, amps[t], turn_slot[(t + 1) % ROW_TILES])
+            tile = held(f"ground{t}", [P, T2], F32)
+            nc.sync.dma_start(tile[:], ground[t * P : (t + 1) * P, :])
+            ground_t.append(tile)
+        w4_raw = load_words("w4_raw", w4_words[0])
+        load_stacked_scales(w4_sc_raw, w4_scales[0].rearrange("r (g c) -> g r c", g=2))
+        b4_t = held("b4_t", [P, 2, 4], F32)
+        nc.sync.dma_start(b4_t[:], b4.rearrange("(g p t) -> p g t", g=2, t=4))
+        v = [gather_words("v_0", tab_win[0], list1, "rounded3")]
+        place_terrain(1, th[1], stage(1, "gained1", [P, S])[:])
+        v.append(gather_words("v_1", tab_win[1], list1))
+        w1_q = [w1_tile(0), w1_tile(1)]
+        place_terrain(2, th[2], stage(2, "gained2", [P, S])[:])
+        phases, amps, angles, weighed = [], [], [], []
+        for t in range(2):
+            phases.append(gate_phase(t, w1_q[t]))
+            amps.append(gate_amplitude(t))
+            angles.append(reduce_phase(t, *phases[t]))
+            weighed.append(weigh_amp(t, amps[t]))
+        w1_q += [w1_tile(2), w1_tile(3)]
+        place_terrain(3, th[3], turn("shifted", "gained3", [P, S], F32, bufs=1)[:])
+        sines = [take_sine(t, angles[t]) for t in range(2)]
+        for t in range(ROW_TILES):
             banks = turn_ground(t)
-            if t + 2 < ROW_TILES:
-                phases.append(gate_phase(t + 2, w1_q[t + 2], turn_slot[t + 2]))
-                amps.append(gate_amplitude(t + 2))
-            nc.vector.tensor_tensor(page_a[:].indirect(list3[:]), sine[:], weighed[:], ALU.mult)
+            ahead = t + 2
+            if ahead < ROW_TILES:
+                phases.append(gate_phase(ahead, w1_q[ahead]))
+                amps.append(gate_amplitude(ahead))
+            nc.vector.tensor_tensor(page_a[:].indirect(list3[:]), sines[t][:], weighed[t][:], ALU.mult)
+            if ahead < ROW_TILES:
+                angles.append(reduce_phase(ahead, *phases[ahead]))
+                weighed.append(weigh_amp(ahead, amps[ahead]))
+                sines.append(take_sine(ahead, angles[ahead]))
             combine(t, banks)
 
-        w4_w = ring.tile([P, N], I32, name="w4_w", tag="work_e", bufs=1, align_bytes=64)
+        w4_w = stage("th2", "w4_w", [P, N], I32)
         nc.vector.tensor_copy(
             w4_w[:].rearrange("p (g t q) -> p g t q", g=2, t=4),
             w4_raw[:].rearrange("p (g q t) -> p g t q", g=2, t=4),
         )
-        w4_sc = ring.tile([P, 512], U8, name="w4_sc", tag="work_s1", bufs=1, align_bytes=64)
+        w4_sc = stage("sine1", "w4_sc", [P, 512], U8)
         nc.vector.tensor_copy(
             w4_sc[:].rearrange("p (t q) -> p t q", t=4),
             w4_sc_raw[:].rearrange("p (q t) -> p t q", t=4),

import math
from contextlib import ExitStack

import concourse.mybir as mybir
from concourse.masks import make_identity

K, H, N, T, T3, S, T2 = 1024, 512, 1024, 2048, 1024, 512, 1024
FLOPS = 2 * (3 * K * H * S + H * N * T2)

F32 = mybir.dt.float32
BF16 = mybir.dt.bfloat16
I32 = mybir.dt.int32
U32 = mybir.dt.uint32
U16 = mybir.dt.uint16
U8 = mybir.dt.uint8
FP8X4 = mybir.dt.float8_e4m3fn_x4
FP4X4 = mybir.dt.float4_e2m1fn_x4
ALU = mybir.AluOpType
ACT = mybir.ActivationFunctionType

P = 128
PASSES = K // 512
ROW_TILES = H // P
HALF = T2 // 2
TWO_PI = 2.0 * math.pi
ROUNDER = 1.5 * 2.0**23


def tile_list_radar_clutter_map_kernel(
    tc, tab_words, tab_scales, tab2_words, tab2_scales, offs, offs2, offs3, offs4,
    w1, w2_words, w2_scales, w3, gain, wg1, wg2, ground, w4_words, w4_scales, b4,
    out_0, out_1, out_2,
):
    nc = tc.nc
    with ExitStack() as ctx:
        lists = ctx.enter_context(tc.tile_pool(name="lists", bufs=1))
        keep = ctx.enter_context(tc.tile_pool(name="keep", bufs=1))
        ring = ctx.enter_context(tc.tile_pool(name="ring", bufs=2))
        psum = ctx.enter_context(tc.psum_pool(name="psum", bufs=1))

        def held(name, shape, dtype):
            return keep.tile(shape, dtype, name=name, align_bytes=64)

        def turn(tag, n, shape, dtype, bufs=2):
            return ring.tile(shape, dtype, name=f"{tag}{n}", tag=tag, bufs=bufs, align_bytes=64)

        def bank(b, name):
            return psum.tile([P, 512], F32, name=name, tag=f"bank{b}")

        def stage(slot, name, shape, dtype=F32):
            return ring.tile(shape, dtype, name=name, tag=f"stage_{slot}", bufs=1, align_bytes=64)

        def load_list(name, src):
            tile = lists.tile([P, S // 16], U16, name=name)
            nc.sync.dma_start(tile[:], src)
            return tile

        def zeroed_bytes(name, shape):
            tile = held(name, shape, U8)
            nc.vector.memset(tile[:].bitcast(I32), 0)
            return tile

        def load_stacked_scales(tile, src, queue=nc.sync):
            for q in range(4):
                queue.dma_start(tile[32 * q : 32 * q + 8, :].bitcast(I32), src[:, 4 * q : 4 * q + 4, :].bitcast(I32))

        def load_words(name, src):
            tile = held(name, [P, src.shape[1]], I32)
            nc.sync.dma_start(tile[:], src.rearrange("p n i -> p (n i)").bitcast(I32))
            return tile

        def gather_words(name, window, offsets, slot=None):
            tile = held(name, [P, S], I32) if slot is None else stage(slot, name, [P, S], I32)
            nc.vector.tensor_copy(tile[:].bitcast(U32), window[:].bitcast(U32).indirect(offsets[:]))
            return tile

        def gather_scales(name, window, offsets, slot=None):
            tile = held(name, [P, S], U8) if slot is None else stage(slot, name, [P, S], U8)
            nc.vector.tensor_copy(tile[:], window[:].indirect(offsets[:]))
            return tile

        def load_weight_columns(tile, w, c0, c1):
            for a in range(PASSES):
                nc.sync.dma_start(
                    tile[:, a, :, :], w[512 * a : 512 * (a + 1), c0:c1].rearrange("(p j) c -> p j c", j=4)
                )

        def quantise_weight(name, rounded):
            codes = held(name + "_codes", [P, PASSES * P], U32)
            scales = held(name + "_scales", [P, PASSES * P], U8)
            nc.vector.quantize_mx(out=codes[:].bitcast(FP8X4), scales=scales[:], in_=rounded[:])
            return codes, scales

        s2_win = zeroed_bytes("s2_win", [P, T3])
        s1_win = zeroed_bytes("s1_win", [P, T])
        page_b = [held(f"page_b{t}", [P, T2], F32) for t in range(ROW_TILES - 1)]
        for page in page_b:
            nc.vector.memset(page[:].bitcast(I32), 0)
        w2_sc = zeroed_bytes("w2_sc", [P, PASSES, H])
        w4_sc_raw = zeroed_bytes("w4_sc_raw", [P, 512])
        v_sc1 = zeroed_bytes("v_sc1", [P, S])
        ident = held("ident", [P, P], F32)
        make_identity(nc, ident[:])

        list2 = load_list("list2", offs2)
        list1 = load_list("list1", offs)
        list4 = load_list("list4", offs4)
        list3 = load_list("list3", offs3)
        tab2_win = [load_words(f"tab2_win{a}", tab2_words[a]) for a in range(PASSES)]
        w3_first = stage("w3_first", "w3_first", [P, PASSES, 4, P])
        load_weight_columns(w3_first, w3, 0, P)
        load_stacked_scales(s2_win, tab2_scales)
        wg2_t = stage("wg2", "wg2_t", [P, S])
        nc.sync.dma_start(wg2_t[:], wg2)
        gain_t = held("gain_t", [P, ROW_TILES], F32)
        with nc.allow_non_contiguous_dma(reason="one gain a partition"):
            nc.sync.dma_start(gain_t[:], gain.rearrange("(t p) -> p t", p=P))
        w3_rest = stage(1, "w3_rest", [P, PASSES, 4, 3 * P])
        load_weight_columns(w3_rest, w3, P, 4 * P)
        load_stacked_scales(s1_win, tab_scales)
        tab_win = [load_words("tab_win0", tab_words[0])]
        w1_raw = [stage(2 + c, f"w1_raw{c}", [P, PASSES, 4, 2 * P]) for c in range(2)]
        load_weight_columns(w1_raw[0], w1, 0, 2 * P)
        tab_win.append(load_words("tab_win1", tab_words[1]))
        load_weight_columns(w1_raw[1], w1, 2 * P, 4 * P)
        w2_w = held("w2_w", [P, PASSES, 2 * H], U8)
        nc.sync.dma_start(w2_w[:].bitcast(I32), w2_words.rearrange("a p c -> p a c").bitcast(I32))
        for q in range(4):
            nc.sync.dma_start(
                w2_sc[32 * q : 32 * q + 4, :, :].bitcast(I32),
                w2_scales[:, 4 * q : 4 * q + 4, :].rearrange("a r c -> r a c").bitcast(I32),
            )

        v2 = [gather_words(f"v2_{a}", tab2_win[a], list2) for a in range(PASSES)]
        v2_sc = gather_scales("v2_sc", s2_win, list2)

        def weight_tile(name, raw, slot):
            rounded = stage(f"rounded{slot}", name + "_bf", [P, 2 * S], BF16)
            dst = rounded[:].rearrange("p (a c i j) -> p a c j i", a=PASSES, i=4, j=4)
            src = raw.rearrange("p a j (c i) -> p a c j i", i=4)
            if name == "w3_0":
                for a in range(PASSES):
                    nc.scalar.activation(dst[:, a], src[:, a], ACT.Copy)
            else:
                nc.scalar.copy(dst, src)
            return quantise_weight(name, rounded)

        def w3_tile(t):
            raw = w3_first[:] if t == 0 else w3_rest[:, :, :, (t - 1) * P : t * P]
            return weight_tile(f"w3_{t}", raw, t)

        def w1_tile(t):
            raw = w1_raw[t // 2][:, :, :, (t % 2) * P : (t % 2 + 1) * P]
            return weight_tile(f"w1_{t}", raw, (1, 4)[t % 2])

        def product(acc, w, moving, moving_scales):
            codes, scales = w
            for a in range(PASSES):
                nc.tensor.matmul_mx(
                    out=acc[:],
                    lhsT=codes[:, a * P : (a + 1) * P].bitcast(FP8X4),
                    lhsT_scale=scales[:, a * P : (a + 1) * P],
                    rhs=moving[a][:].bitcast(FP8X4),
                    rhs_scale=moving_scales[4 * a : P, :],
                    start=(a == 0),
                    stop=(a == PASSES - 1),
                )

        def terrain_tanh(t, w3_q):
            pre = bank(t % 2, f"pre{t}")
            product(pre, w3_q, v2, v2_sc)
            th = stage(f"th{t}", f"th{t}", [P, S])
            nc.scalar.activation(th[:], pre[:], ACT.Tanh)
            return th

        def place_terrain(t, th, gained):
            nc.scalar.activation(gained, wg2_t[:], ACT.Copy, scale=gain_t[:, t : t + 1])
            nc.vector.tensor_tensor(page_b[t][:].indirect(list4[:]), th[:], gained, ALU.mult)

        th = [terrain_tanh(0, w3_tile(0))]
        page_b.append(stage("rounded0", "page_b3", [P, T2]))
        page_a = stage("w3_first", "page_a", [P, T2])
        for page in (page_b[3], page_a):
            nc.vector.memset(page[:].bitcast(I32), 0)

        def gate_amplitude(t):
            amp = bank(4 + t % 2, f"amp{t}")
            for a in range(PASSES):
                nc.tensor.matmul_mx(
                    out=amp[:],
                    lhsT=w2_w[:, a, 2 * P * t : 2 * P * (t + 1)].bitcast(FP4X4),
                    lhsT_scale=w2_sc[:, a, P * t : P * (t + 1)],
                    rhs=v[a][:].bitcast(FP8X4),
                    rhs_scale=(v_sc if a == 0 else v_sc1)[:],
                    start=(a == 0),
                    stop=(a == PASSES - 1),
                )
            return amp

        def gate_phase(t, w1_q):
            phase = bank(2 + t % 2, f"phase{t}")
            product(phase, w1_q, v, v_sc)
            shifted = turn("shifted", t, [P, S], U32, bufs=1)
            nc.scalar.activation(shifted[:], phase[:], ACT.Copy, bias=ROUNDER, scale=1.0 / TWO_PI)
            turns = turn("turns", t, [P, S], F32)
            nc.scalar.activation(turns[:], shifted[:], ACT.Copy, bias=-ROUNDER, scale=1.0)
            return phase, turns

        def reduce_phase(t, phase, turns):
            angle = turn("angle", t, [P, S], F32)
            nc.vector.scalar_tensor_tensor(angle[:], turns[:], -TWO_PI, phase[:], ALU.mult, ALU.add)
            return angle

        def take_sine(t, angle):
            sine = stage("wg2" if t == 0 else f"sine{t % 2}", f"sine{t}", [P, S])
            nc.scalar.activation(sine[:], angle[:], ACT.Sin)
            return sine

        def weigh_amp(t, amp):
            weighed = stage((2, "th2")[t % 2], f"weighed{t}", [P, S])
            nc.vector.tensor_tensor(weighed[:], amp[:], wg1_t[:], ALU.mult)
            return weighed

        z_turned = [held(f"z_turned{h}", [P, 4 * HALF], BF16) for h in range(2)]

        def turn_ground(t):
            banks = []
            for h in range(2):
                acc = bank((6 if t % 2 == 0 else 0) + h, f"zt{t}_{h}")
                for b in range(4):
                    cols = slice(h * HALF + b * P, h * HALF + (b + 1) * P)
                    nc.tensor.matmul(
                        acc[:, b * P : (b + 1) * P], ground_t[t][:, cols], ident[:],
                        start=(b == 0), stop=False, is_transpose=True,
                    )
                banks.append(acc)
            return banks

        def combine(t, banks):
            larger = turn("larger", t, [P, T2], F32)
            last = t == ROW_TILES - 1
            if not last:
                nc.vector.tensor_tensor(larger[:], page_a[:], page_b[t][:], ALU.max)
            for h in range(2):
                cols = slice(h * HALF, (h + 1) * HALF)
                if last:
                    nc.vector.tensor_tensor(larger[:, cols], page_a[:, cols], page_b[t][:, cols], ALU.max)
                acc = banks[h]
                for b in range(4):
                    nc.tensor.matmul(
                        acc[:, b * P : (b + 1) * P], larger[:, h * HALF + b * P : h * HALF + (b + 1) * P], ident[:],
                        start=False, stop=(b == 3), is_transpose=True,
                    )
                nc.scalar.copy(
                    z_turned[h][:].rearrange("p (b u q e) -> p b u q e", b=4, u=2, e=2)[:, :, :, 32 * t : 32 * (t + 1), :],
                    acc[:].rearrange("p (b q u e) -> p b u q e", b=4, u=2, e=2),
                )

        place_terrain(0, th[0], held("gained0", [P, S], F32)[:])
        for t in range(1, ROW_TILES):
            th.append(terrain_tanh(t, w3_tile(t)))
        v_sc = gather_scales("v_sc", s1_win, list1, "rounded2")
        nc.sync.dma_start(v_sc1[0:100, :].bitcast(I32), v_sc[4:104, :].bitcast(I32))
        wg1_t = held("wg1_t", [P, S], F32)
        nc.sync.dma_start(wg1_t[:], wg1)
        ground_t = []
        for t in range(ROW_TILES):
            tile = held(f"ground{t}", [P, T2], F32)
            nc.sync.dma_start(tile[:], ground[t * P : (t + 1) * P, :])
            ground_t.append(tile)
        w4_raw = load_words("w4_raw", w4_words[0])
        load_stacked_scales(w4_sc_raw, w4_scales[0].rearrange("r (g c) -> g r c", g=2))
        b4_t = held("b4_t", [P, 2, 4], F32)
        nc.sync.dma_start(b4_t[:], b4.rearrange("(g p t) -> p g t", g=2, t=4))
        v = [gather_words("v_0", tab_win[0], list1, "rounded3")]
        place_terrain(1, th[1], stage(1, "gained1", [P, S])[:])
        v.append(gather_words("v_1", tab_win[1], list1))
        w1_q = [w1_tile(0), w1_tile(1)]
        place_terrain(2, th[2], stage(2, "gained2", [P, S])[:])
        phases, amps, angles, weighed = [], [], [], []
        for t in range(2):
            phases.append(gate_phase(t, w1_q[t]))
            amps.append(gate_amplitude(t))
            angles.append(reduce_phase(t, *phases[t]))
            weighed.append(weigh_amp(t, amps[t]))
        w1_q += [w1_tile(2), w1_tile(3)]
        place_terrain(3, th[3], turn("shifted", "gained3", [P, S], F32, bufs=1)[:])
        sines = [take_sine(t, angles[t]) for t in range(2)]
        for t in range(ROW_TILES):
            banks = turn_ground(t)
            ahead = t + 2
            if ahead < ROW_TILES:
                phases.append(gate_phase(ahead, w1_q[ahead]))
                amps.append(gate_amplitude(ahead))
            nc.vector.tensor_tensor(page_a[:].indirect(list3[:]), sines[t][:], weighed[t][:], ALU.mult)
            if ahead < ROW_TILES:
                angles.append(reduce_phase(ahead, *phases[ahead]))
                weighed.append(weigh_amp(ahead, amps[ahead]))
                sines.append(take_sine(ahead, angles[ahead]))
            combine(t, banks)

        w4_w = stage("th2", "w4_w", [P, N], I32)
        nc.vector.tensor_copy(
            w4_w[:].rearrange("p (g t q) -> p g t q", g=2, t=4),
            w4_raw[:].rearrange("p (g q t) -> p g t q", g=2, t=4),
        )
        w4_sc = stage("sine1", "w4_sc", [P, 512], U8)
        nc.vector.tensor_copy(
            w4_sc[:].rearrange("p (t q) -> p t q", t=4),
            w4_sc_raw[:].rearrange("p (q t) -> p t q", t=4),
        )

        def quantise_z(h):
            words = z_turned[h][:].bitcast(F32)
            z_in = held(f"z_in{h}", [P, 4 * HALF], BF16)
            for d in range(2):
                acc = bank(2 + 2 * h + d, f"zback{h}_{d}")
                for s in range(4):
                    nc.tensor.transpose(
                        acc[:, s * P : (s + 1) * P], words[:, (4 * d + s) * P : (4 * d + s + 1) * P], ident[:]
                    )
                dst = z_in[:].bitcast(F32)[:, 512 * d : 512 * (d + 1)].rearrange("p (b m u) -> p b m u", b=2, u=2)
                src = acc[:].rearrange("p (b u m) -> p b m u", b=2, u=2)
                if d == 0:
                    nc.vector.tensor_copy(dst, src)
                else:
                    nc.scalar.copy(dst, src)
            codes = held(f"z_codes{h}", [P, HALF], U32)
            scales = held(f"z_scales{h}", [P, HALF], U8)
            nc.vector.quantize_mx(out=codes[:].bitcast(FP8X4), scales=scales[:], in_=z_in[:])
            return codes, scales

        z_q = [quantise_z(h) for h in range(2)]

        out_rows = out_0.rearrange("(g p t) m -> g p t m", g=2, t=4)
        y_scales = held("y_scales", [P, 2, T2], U8)
        for h in range(2):
            cols = slice(h * HALF, (h + 1) * HALF)
            for g in range(2):
                unit = 2 * h + g
                y = stage(unit, f"y{unit}", [P, 4, HALF])
                for t in range(4):
                    acc = bank((6 + 4 * unit + t) % 8, f"y{unit}_{t}")
                    nc.tensor.matmul_mx(
                        out=acc[:],
                        lhsT=w4_w[:, (4 * g + t) * P : (4 * g + t + 1) * P].bitcast(FP8X4),
                        lhsT_scale=w4_sc[4 * g : P, t * P : (t + 1) * P],
                        rhs=z_q[h][0][:].bitcast(FP8X4),
                        rhs_scale=z_q[h][1][:],
                        start=True,
                        stop=True,
                    )
                    bias = b4_t[:, g, t : t + 1]
                    if unit == 0 and t % 2 == 1:
                        nc.vector.tensor_scalar(y[:, t, :], acc[:], bias, None, ALU.add)
                    else:
                        nc.scalar.activation(y[:, t, :], acc[:], ACT.Identity, bias=bias)
                    if unit == 0:
                        nc.sync.dma_start(out_rows[g][:, t, cols], y[:, t, :])
                    elif t % 2 == 1:
                        nc.sync.dma_start(out_rows[g][:, t - 1 : t + 1, cols], y[:, t - 1 : t + 1, :])
                y_bf = turn("y_bf", unit, [P, 4 * HALF], BF16)
                nc.vector.tensor_copy(
                    y_bf[:].rearrange("p (c i t) -> p c t i", i=4, t=4),
                    y[:].rearrange("p t (c i) -> p c t i", i=4),
                )
                y_codes = held(f"y_codes{unit}", [P, HALF], I32)
                nc.vector.quantize_mx(out=y_codes[:].bitcast(FP8X4), scales=y_scales[:, g, cols], in_=y_bf[:])
                nc.sync.dma_start(out_1[g][:, cols, :].rearrange("p m i -> p (m i)").bitcast(I32), y_codes[:])
        for q in range(4):
            nc.sync.dma_start(
                out_2[:, 4 * q : 4 * q + 4, :].rearrange("g r c -> r g c").bitcast(I32),
                y_scales[32 * q : 32 * q + 4, :, :].bitcast(I32),
            )
